import numpy as np, ml_dtypes
CORES = [4,20,36,44,92,100,108,116,3,19,35,43,91,99,107,115]
N = 16
import mx_ref
NC, G = 128, 4
C = np.float32(0.019)
BF = ml_dtypes.bfloat16
def tile(rs):
    return np.stack(rs, axis=2).reshape(128, -1).astype(BF)
def act(Z):
    return [np.maximum(z, 0) * C for z in Z]
def pk(c, s, i=0):
    return (np.ascontiguousarray(c[:, 512 * i:512 * i + 512]), mx_ref.live(s[:, 128 * i:128 * i + 128]))
def inputs(rng, e, E):
    def f(*shape):
        v = (rng.standard_normal(shape, dtype=np.float32) * np.exp2(rng.integers(-2, 3, shape[:-1] + (1,)))).astype(BF)
        return mx_ref.spread((v.astype(np.float32) * np.exp2(rng.integers(-E, E + 1, shape[:-2] + (1, 1))).astype(np.float32)).astype(BF), rng, e)
    def packed(k):
        c = np.zeros((N, 128, k * 512), np.uint8); s = np.zeros((N, 128, k * 128), np.uint8)
        for r in range(N):
            for i in range(k):
                a, b = mx_ref.quantize(f(128, 512)); c[r][:, 512 * i:512 * i + 512] = a; s[r][:, 128 * i:128 * i + 128] = mx_ref.plane(b, rng)
        return c, s
    d = {}
    d["ac"], d["az"] = packed(1)
    d["bc"], d["bs"] = packed(1)
    d["x"] = f(N, 128, 4 * NC)
    return d
def setup_inputs(rng):
    return inputs(rng, 0, 0)
def setup_inputs_blocks(rng):
    return inputs(rng, 4, 0)
def setup_inputs_wide(rng):
    return inputs(rng, 0, 8)
def reference(ac, az, bc, bs, x):
    y = np.zeros((N, 128, N * NC), np.float32)
    for r in range(N):
        X = mx_ref.quantize(x[r])
        h = mx_ref.quantize(tile(act([mx_ref.matmul(pk(ac[i], az[i]), X) for i in range(G)])))
        for j in range(N):
            y[r][:, NC * j:NC * j + NC] = mx_ref.matmul(pk(bc[j], bs[j]), h)
    return {"y": y}

@@ -1,0 +1,297 @@
+from concourse.bass import DstId, RemoteDMATransfer
+from concourse.mybir import dt, AluOpType, ActivationFunctionType
+
+NA, NB, W = 4, 16, 128
+NT = NA + NB
+CSCALE = 0.019
+PEN = 4
+FWD = 16
+
+SCRATCH = {
+    "wc": ("sbuf", [128, NT * W], "float8_e4m3fn_x4"),
+    "ws": ("sbuf", [128, NT * W], "uint8"),
+    "xt": ("sbuf", [128, 4 * W], "bfloat16"),
+    "xq": ("sbuf", [128, W], "float8_e4m3fn_x4"),
+    "xs": ("sbuf", [128, W], "uint8"),
+    "ht": ("sbuf", [128, 4 * W], "bfloat16"),
+    "hq": ("sbuf", [128, W], "float8_e4m3fn_x4"),
+    "hs": ("sbuf", [128, W], "uint8"),
+    "yo": ("sbuf", [128, NB * W], "float32"),
+    "ps": ("psum", [128, 8 * 512], "float32"),
+}
+for _t in range(NT):
+    SCRATCH["dc%d" % _t] = ("dram", [128, W], "float8_e4m3fn_x4")
+    SCRATCH["dp%d" % _t] = ("dram", [128, W], "uint8")
+
+SEMAPHORES = (["S%d" % t for t in range(NT)] + ["D%d" % t for t in range(NT)]
+              + ["z%d" % i for i in range(NA)] + ["m%d" % j for j in range(NB)] + ["e%d" % j for j in range(NB)]
+              + ["lsem", "xl", "xqd", "act", "hqd", "st"])
+
+_CACHE = {}
+
+
+def _plan(cores, topo):
+    ncore = topo.CHIPS * topo.CORES_PER_CHIP
+    rank = {c: i for i, c in enumerate(cores)}
+    chips, R = [], {}
+    for c in cores:
+        if topo.chip(c) not in chips:
+            chips.append(topo.chip(c))
+        R[(topo.chip(c), topo.die(c))] = c
+    d0 = topo.die(cores[0])
+    dies = [d0, 1 - d0]
+    pl0 = [ch for ch in chips if ch == chips[0] or topo.same_plane(ch, chips[0])]
+    planes = [pl0, [ch for ch in chips if ch not in pl0]]
+    plane_of = {ch: k for k, pl in enumerate(planes) for ch in pl}
+
+    slot, groups, blk = {}, {}, {}
+    s = NA
+    for d in dies:
+        for k, pl in enumerate(planes):
+            groups[(d, k)] = (s, len(pl))
+            for ch in pl:
+                slot[rank[R[(ch, d)]]] = s
+                blk[s] = rank[R[(ch, d)]]
+                s += 1
+
+    ops, avail, loads, load = {}, {}, {}, {}
+
+    def helpers(ch, d):
+        return [c for c in range(ncore) if topo.chip(c) == ch and topo.die(c) == d and c not in rank]
+
+    def ring(ch):
+        i = chips.index(ch)
+        return [chips[(i + k) % len(chips)] for k in range(1, len(chips))]
+
+    def add(src, prio, s0, n, parts):
+        parts = [p for p in parts if p[2]]
+        if not parts:
+            return
+        ops.setdefault(src, [])
+        ops[src].append((prio, len(ops[src]), s0, n, parts))
+        for (sm, dm, dsts, lo, ne) in parts:
+            for dst in dsts:
+                for t in range(s0, s0 + n):
+                    avail[(dst, t, dm)] = (dm + str(s0), 2 * ne)
+
+    def share(dsts, cands):
+        out = {c: [] for c in cands}
+        for dst in dsts:
+            best = None
+            for c in cands:
+                if c not in load:
+                    load[c] = PEN
+                if best is None or load[c] < load[best]:
+                    best = c
+            out[best].append(dst)
+            load[best] += 1
+        return out
+
+    def gates(ch, d, dsts):
+        return [c for c in helpers(ch, d) + [R[(ch, d)]] if all(topo.may_write(c, x) for x in dsts)]
+
+    for c in cores:
+        load[c] = len([c2 for c2 in chips if topo.same_plane(topo.chip(c), c2)])
+
+    landed = {}
+    for i in range(NA):
+        o = cores[i]
+        ch, d = topo.chip(o), topo.die(o)
+        sib = R[(ch, 1 - d)]
+        same = [c2 for c2 in ring(ch) if topo.same_plane(ch, c2)]
+        crs = [c2 for c2 in ring(ch) if not topo.same_plane(ch, c2)]
+        direct = [R[(c2, d)] for c2 in same]
+        load[o] += len(direct)
+        for x in direct:
+            landed.setdefault(x, []).append(i)
+        feed = []
+        for pd in (d, 1 - d):
+            dsts = [R[(c2, pd)] for c2 in crs]
+            for c, lst in share(dsts, gates(ch, pd, dsts)).items():
+                if not lst:
+                    continue
+                if c == o:
+                    direct = direct + lst
+                elif c == sib:
+                    add(sib, 2, i, 1, [("S", "S", lst, 0, 8)])
+                else:
+                    feed.append(c)
+                    add(c, 2, i, 1, [("D", "S", lst, 0, 8)])
+        loads.setdefault(o, []).append((i, "a", "S"))
+        avail[(o, i, "S")] = ("S%d" % i, 32)
+        if feed:
+            loads[o].append((i, "a", "D"))
+            avail[(o, i, "D")] = ("D%d" % i, 32)
+        add(o, 0, i, 1, [("S", "S", direct, 0, 8), ("S", "S", [sib], 8, 4), ("D", "D", feed, 12, 4)])
+
+    for x, got in landed.items():
+        sib = R[(topo.chip(x), 1 - topo.die(x))]
+        got = sorted(got)
+        a = 0
+        while a < len(got):
+            b = a
+            while b + 1 < len(got) and got[b + 1] == got[b] + 1:
+                b += 1
+            add(x, 4, got[a], b - a + 1, [("S", "S", [sib], 0, FWD)])
+            a = b + 1
+
+    for j, o in enumerate(cores):
+        t = slot[j]
+        ch, d = topo.chip(o), topo.die(o)
+        direct = [R[(c2, d)] for c2 in ring(ch) if topo.same_plane(ch, c2)]
+        dsts = [R[(c2, d)] for c2 in ring(ch) if not topo.same_plane(ch, c2)]
+        feed = []
+        sh = share(dsts, gates(ch, d, dsts))
+        for h in helpers(ch, d):
+            while direct and load.get(h, PEN) + 1 < load[o]:
+                load[h] = load.get(h, PEN) + 1
+                load[o] -= 1
+                sh.setdefault(h, []).append(direct.pop())
+        for c, lst in sh.items():
+            if not lst:
+                continue
+            if c == o:
+                direct = direct + lst
+            else:
+                feed.append(c)
+                add(c, 3, t, 1, [("D", "S", lst, 0, 8)])
+        loads.setdefault(o, []).append((t, "b", "S"))
+        avail[(o, t, "S")] = ("S%d" % t, 32)
+        if feed:
+            loads[o].append((t, "b", "D"))
+            avail[(o, t, "D")] = ("D%d" % t, 32)
+        add(o, 1, t, 1, [("S", "S", direct, 0, 8), ("D", "D", feed, 8, 8)])
+
+    waves, aorder = {}, {}
+    for o in cores:
+        ch, d = topo.chip(o), topo.die(o)
+        k = plane_of[ch]
+        sib = R[(ch, 1 - d)]
+        add(o, 5, groups[(d, k)][0], groups[(d, k)][1], [("S", "S", [sib], 0, FWD)])
+        add(o, 6, groups[(d, 1 - k)][0], groups[(d, 1 - k)][1], [("S", "S", [sib], 0, FWD)])
+        waves[o] = [groups[(d, k)], groups[(d, 1 - k)], groups[(1 - d, k)], groups[(1 - d, 1 - k)]]
+        aorder[o] = sorted(range(NA), key=lambda i: (plane_of[topo.chip(cores[i])] != k, i))
+    return {"ops": ops, "avail": avail, "loads": loads, "waves": waves, "aorder": aorder, "blk": blk}
+
+
+def rank_program(g, core, T, topo):
+    key = tuple(T.cores)
+    if key not in _CACHE:
+        _CACHE[key] = _plan(list(T.cores), topo)
+    P = _CACHE[key]
+    avail = P["avail"]
+    u8 = dt.uint8
+
+    def codes(m, s0, n):
+        if m == "S":
+            return T.wc[:, s0 * W:(s0 + n) * W].bitcast(u8)
+        return T["dc%d" % s0][:].bitcast(u8)
+
+    def plane(m, s0, n):
+        if m == "S":
+            return T.ws[:, s0 * W:(s0 + n) * W]
+        return T["dp%d" % s0][:]
+
+    def engines(dsts, lo, ne):
+        ok = None
+        for x in dsts:
+            ok = topo.mask(core, x) if ok is None else ok & topo.mask(core, x)
+        bits = [b for b in range(16) if (ok >> b) & 1][lo:lo + ne]
+        return sum(1 << b for b in bits)
+
+    rank = T.rank_of(core)
+    if rank is not None:
+        src = {"a": (T.ac, T.az), "b": (T.bc, T.bs)}
+        has_a = any(k == "a" for (_, k, _) in P["loads"][core])
+        for (t, k, m) in P["loads"][core]:
+            q = g.scalar if (has_a and k == "b") else g.sync
+            q.dma_start(codes(m, t, 1), src[k][0][:, :]).then_inc(T.sem[m + str(t)], 16)
+            q.dma_start(plane(m, t, 1), src[k][1][:, :]).then_inc(T.sem[m + str(t)], 16)
+        g.scalar.dma_start(T.xt[:], T.x[:, :]).then_inc(T.sem.xl, 16)
+
+    seen, lcount = set(), 0
+    for (prio, seq, s0, n, parts) in sorted(P["ops"].get(core, [])):
+        for (sm, dm, dsts, lo, ne) in parts:
+            for t in range(s0, s0 + n):
+                sem, cnt = avail[(core, t, sm)]
+                if sem not in seen:
+                    seen.add(sem)
+                    g.wait_ge(T.sem[sem], cnt)
+        for view in (plane, codes):
+            trs = []
+            for (sm, dm, dsts, lo, ne) in parts:
+                ids = []
+                for x in dsts:
+                    rid, pid, _se = topo.addr(x)
+                    ids.append(DstId(rid=rid, pnc=pid))
+                trs.append(RemoteDMATransfer(dst_ids=ids, dma_engine_mask=engines(dsts, lo, ne),
+                                             remote_sem=T.sem[dm + str(s0)], srcs=[view(sm, s0, n)],
+                                             dsts=[view(dm, s0, n) for _x in dsts]))
+                lcount += ne
+            g.remote_dma_fused(trs, local_sem=T.sem.lsem)
+    if lcount:
+        g.wait_ge(T.sem.lsem, lcount)
+    if rank is None:
+        return
+
+    v, sc, te = g.vector, g.scalar, g.tensor
+    v.wait_ge(T.sem.xl, 16)
+    v.quantize_mx(T.xq[:], T.xs[:], T.xt[:]).then_inc(T.sem.xqd, 1)
+    te.wait_ge(T.sem.xqd, 1)
+    tseen = set()
+
+    def twait(t):
+        sem, cnt = avail[(core, t, "S")]
+        if sem not in tseen:
+            tseen.add(sem)
+            te.wait_ge(T.sem[sem], cnt)
+
+    for n_, i in enumerate(P["aorder"][core]):
+        twait(i)
+        te.matmul_mx(T.ps[:, i * 512:i * 512 + W], T.wc[:, i * W:(i + 1) * W], T.ws[:, i * W:(i + 1) * W],
+                     T.xq[:], T.xs[:], True, True).then_inc(T.sem["z%d" % i], 1)
+        if n_ % 2 == 0:
+            v.wait_ge(T.sem["z%d" % i], 1)
+            v.tensor_scalar(T.ht[:, i:4 * W:4], T.ps[:, i * 512:i * 512 + W], 0.0, CSCALE,
+                            AluOpType.max, AluOpType.mult).then_inc(T.sem.act, 1)
+        else:
+            sc.wait_ge(T.sem["z%d" % i], 1)
+            sc.activation(T.ht[:, i:4 * W:4], T.ps[:, i * 512:i * 512 + W], ActivationFunctionType.Relu,
+                          scale=CSCALE).then_inc(T.sem.act, 1)
+    v.wait_ge(T.sem.act, NA)
+    v.quantize_mx(T.hq[:], T.hs[:], T.ht[:]).then_inc(T.sem.hqd, 1)
+    te.wait_ge(T.sem.hqd, 1)
+
+    order, nst = [], 0
+    for (s0, n) in P["waves"][core]:
+        js = []
+        for t in range(s0, s0 + n):
+            j = P["blk"][t]
+            k = len(order)
+            bank = (NA + k) % 8
+            twait(t)
+            if k >= 8:
+                te.wait_ge(T.sem["e%d" % order[k - 8]], 1)
+            te.matmul_mx(T.ps[:, bank * 512:bank * 512 + W], T.wc[:, t * W:(t + 1) * W], T.ws[:, t * W:(t + 1) * W],
+                         T.hq[:], T.hs[:], True, True).then_inc(T.sem["m%d" % j], 1)
+            if k % 2 == 0:
+                v.wait_ge(T.sem["m%d" % j], 1)
+                v.tensor_copy(T.yo[:, j * W:(j + 1) * W], T.ps[:, bank * 512:bank * 512 + W]).then_inc(T.sem["e%d" % j], 1)
+            else:
+                sc.wait_ge(T.sem["m%d" % j], 1)
+                sc.activation(T.yo[:, j * W:(j + 1) * W], T.ps[:, bank * 512:bank * 512 + W],
+                              ActivationFunctionType.Copy).then_inc(T.sem["e%d" % j], 1)
+            order.append(j)
+            js.append(j)
+        js.sort()
+        a = 0
+        while a < len(js):
+            b = a
+            while b + 1 < len(js) and js[b + 1] == js[b] + 1:
+                b += 1
+            for j in js[a:b + 1]:
+                g.sync.wait_ge(T.sem["e%d" % j], 1)
+            g.sync.dma_start(T.y[:, js[a] * W:(js[b] + 1) * W], T.yo[:, js[a] * W:(js[b] + 1) * W]).then_inc(T.sem.st, 16)
+            nst += 1
+            a = b + 1
+    g.sync.wait_ge(T.sem.st, 16 * nst)

@@ -23,7 +23,7 @@ for _t in range(NT):
     SCRATCH["dc%d" % _t] = ("dram", [128, W], "float8_e4m3fn_x4")
     SCRATCH["dp%d" % _t] = ("dram", [128, W], "uint8")
 
-SEMAPHORES = (["S%d" % t for t in range(NT)] + ["D%d" % t for t in range(NT)]
+SEMAPHORES = (["%s%s%d" % (v, m, t) for v in "pc" for m in "SD" for t in range(NT)]
               + ["z%d" % i for i in range(NA)] + ["m%d" % j for j in range(NB)] + ["e%d" % j for j in range(NB)]
               + ["lsem", "xl", "xqd", "act", "hqd", "st"])
 
@@ -72,7 +72,7 @@ def _plan(cores, topo):
         for (sm, dm, dsts, lo, ne) in parts:
             for dst in dsts:
                 for t in range(s0, s0 + n):
-                    avail[(dst, t, dm)] = (dm + str(s0), 2 * ne)
+                    avail[(dst, t, dm)] = (dm + str(s0), ne)
 
     def share(dsts, cands):
         out = {c: [] for c in cands}
@@ -117,12 +117,10 @@ def _plan(cores, topo):
                 else:
                     feed.append(c)
                     add(c, 2, i, 1, [("D", "S", lst, 0, 8)])
-        loads.setdefault(o, []).append((i, "a", "S"))
-        avail[(o, i, "S")] = ("S%d" % i, 32)
-        if feed:
-            loads[o].append((i, "a", "D"))
-            avail[(o, i, "D")] = ("D%d" % i, 32)
-        add(o, 0, i, 1, [("S", "S", direct, 0, 8), ("S", "S", [sib], 8, 4), ("D", "D", feed, 12, 4)])
+        loads.setdefault(o, []).append((i, "a"))
+        avail[(o, i, "S")] = ("S%d" % i, 16)
+        avail[(o, i, "D")] = ("D%d" % i, 16)
+        add(o, 0, i, 1, [("D", "S", direct, 0, 8), ("D", "S", [sib], 8, 4), ("D", "D", feed, 12, 4)])
 
     for x, got in landed.items():
         sib = R[(topo.chip(x), 1 - topo.die(x))]
@@ -155,12 +153,10 @@ def _plan(cores, topo):
             else:
                 feed.append(c)
                 add(c, 3, t, 1, [("D", "S", lst, 0, 8)])
-        loads.setdefault(o, []).append((t, "b", "S"))
-        avail[(o, t, "S")] = ("S%d" % t, 32)
-        if feed:
-            loads[o].append((t, "b", "D"))
-            avail[(o, t, "D")] = ("D%d" % t, 32)
-        add(o, 1, t, 1, [("S", "S", direct, 0, 8), ("D", "D", feed, 8, 8)])
+        loads.setdefault(o, []).append((t, "b"))
+        avail[(o, t, "S")] = ("S%d" % t, 16)
+        avail[(o, t, "D")] = ("D%d" % t, 16)
+        add(o, 1, t, 1, [("D", "S", direct, 0, 8), ("D", "D", feed, 8, 8)])
 
     waves, aorder = {}, {}
     for o in cores:
@@ -202,22 +198,24 @@ def rank_program(g, core, T, topo):
     rank = T.rank_of(core)
     if rank is not None:
         src = {"a": (T.ac, T.az), "b": (T.bc, T.bs)}
-        has_a = any(k == "a" for (_, k, _) in P["loads"][core])
-        for (t, k, m) in P["loads"][core]:
-            q = g.scalar if (has_a and k == "b") else g.sync
-            q.dma_start(codes(m, t, 1), src[k][0][:, :]).then_inc(T.sem[m + str(t)], 16)
-            q.dma_start(plane(m, t, 1), src[k][1][:, :]).then_inc(T.sem[m + str(t)], 16)
+        for (t, k) in P["loads"][core]:
+            g.sync.dma_start(plane("D", t, 1), src[k][1][:, :]).then_inc(T.sem["pD%d" % t], 16)
+            g.scalar.dma_start(codes("D", t, 1), src[k][0][:, :]).then_inc(T.sem["cD%d" % t], 16)
         g.scalar.dma_start(T.xt[:], T.x[:, :]).then_inc(T.sem.xl, 16)
+        for n_, (t, k) in enumerate(P["loads"][core]):
+            q = g.sync if n_ == 0 else g.scalar
+            q.dma_start(codes("S", t, 1), src[k][0][:, :]).then_inc(T.sem["cS%d" % t], 16)
+            g.sync.dma_start(plane("S", t, 1), src[k][1][:, :]).then_inc(T.sem["pS%d" % t], 16)
 
     seen, lcount = set(), 0
     for (prio, seq, s0, n, parts) in sorted(P["ops"].get(core, [])):
-        for (sm, dm, dsts, lo, ne) in parts:
-            for t in range(s0, s0 + n):
-                sem, cnt = avail[(core, t, sm)]
-                if sem not in seen:
-                    seen.add(sem)
-                    g.wait_ge(T.sem[sem], cnt)
-        for view in (plane, codes):
+        for (vn, view) in (("p", plane), ("c", codes)):
+            for (sm, dm, dsts, lo, ne) in parts:
+                for t in range(s0, s0 + n):
+                    sem, cnt = avail[(core, t, sm)]
+                    if vn + sem not in seen:
+                        seen.add(vn + sem)
+                        g.wait_ge(T.sem[vn + sem], cnt)
             trs = []
             for (sm, dm, dsts, lo, ne) in parts:
                 ids = []
@@ -225,7 +223,7 @@ def rank_program(g, core, T, topo):
                     rid, pid, _se = topo.addr(x)
                     ids.append(DstId(rid=rid, pnc=pid))
                 trs.append(RemoteDMATransfer(dst_ids=ids, dma_engine_mask=engines(dsts, lo, ne),
-                                             remote_sem=T.sem[dm + str(s0)], srcs=[view(sm, s0, n)],
+                                             remote_sem=T.sem[vn + dm + str(s0)], srcs=[view(sm, s0, n)],
                                              dsts=[view(dm, s0, n) for _x in dsts]))
                 lcount += ne
             g.remote_dma_fused(trs, local_sem=T.sem.lsem)
@@ -244,7 +242,8 @@ def rank_program(g, core, T, topo):
         sem, cnt = avail[(core, t, "S")]
         if sem not in tseen:
             tseen.add(sem)
-            te.wait_ge(T.sem[sem], cnt)
+            te.wait_ge(T.sem["p" + sem], cnt)
+            te.wait_ge(T.sem["c" + sem], cnt)
 
     for n_, i in enumerate(P["aorder"][core]):
         twait(i)

from concourse.bass import DstId, RemoteDMATransfer
from concourse.mybir import dt, AluOpType, ActivationFunctionType

NA, NB, W = 4, 16, 128
NT = NA + NB
CSCALE = 0.019
PEN = 4
FWD = 16

SCRATCH = {
    "wc": ("sbuf", [128, NT * W], "float8_e4m3fn_x4"),
    "ws": ("sbuf", [128, NT * W], "uint8"),
    "xt": ("sbuf", [128, 4 * W], "bfloat16"),
    "xq": ("sbuf", [128, W], "float8_e4m3fn_x4"),
    "xs": ("sbuf", [128, W], "uint8"),
    "ht": ("sbuf", [128, 4 * W], "bfloat16"),
    "hq": ("sbuf", [128, W], "float8_e4m3fn_x4"),
    "hs": ("sbuf", [128, W], "uint8"),
    "yo": ("sbuf", [128, NB * W], "float32"),
    "ps": ("psum", [128, 8 * 512], "float32"),
}
for _t in range(NT):
    SCRATCH["dc%d" % _t] = ("dram", [128, W], "float8_e4m3fn_x4")
    SCRATCH["dp%d" % _t] = ("dram", [128, W], "uint8")

SEMAPHORES = (["%s%s%d" % (v, m, t) for v in "pc" for m in "SD" for t in range(NT)]
              + ["z%d" % i for i in range(NA)] + ["m%d" % j for j in range(NB)] + ["e%d" % j for j in range(NB)]
              + ["lsem", "xl", "xqd", "act", "hqd", "st"])

_CACHE = {}


def _plan(cores, topo):
    ncore = topo.CHIPS * topo.CORES_PER_CHIP
    rank = {c: i for i, c in enumerate(cores)}
    chips, R = [], {}
    for c in cores:
        if topo.chip(c) not in chips:
            chips.append(topo.chip(c))
        R[(topo.chip(c), topo.die(c))] = c
    d0 = topo.die(cores[0])
    dies = [d0, 1 - d0]
    pl0 = [ch for ch in chips if ch == chips[0] or topo.same_plane(ch, chips[0])]
    planes = [pl0, [ch for ch in chips if ch not in pl0]]
    plane_of = {ch: k for k, pl in enumerate(planes) for ch in pl}

    slot, groups, blk = {}, {}, {}
    s = NA
    for d in dies:
        for k, pl in enumerate(planes):
            groups[(d, k)] = (s, len(pl))
            for ch in pl:
                slot[rank[R[(ch, d)]]] = s
                blk[s] = rank[R[(ch, d)]]
                s += 1

    ops, avail, loads, load = {}, {}, {}, {}

    def helpers(ch, d):
        return [c for c in range(ncore) if topo.chip(c) == ch and topo.die(c) == d and c not in rank]

    def ring(ch):
        i = chips.index(ch)
        return [chips[(i + k) % len(chips)] for k in range(1, len(chips))]

    def add(src, prio, s0, n, parts):
        parts = [p for p in parts if p[2]]
        if not parts:
            return
        ops.setdefault(src, [])
        ops[src].append((prio, len(ops[src]), s0, n, parts))
        for (sm, dm, dsts, lo, ne) in parts:
            for dst in dsts:
                for t in range(s0, s0 + n):
                    avail[(dst, t, dm)] = (dm + str(s0), ne)

    def share(dsts, cands):
        out = {c: [] for c in cands}
        for dst in dsts:
            best = None
            for c in cands:
                if c not in load:
                    load[c] = PEN
                if best is None or load[c] < load[best]:
                    best = c
            out[best].append(dst)
            load[best] += 1
        return out

    def gates(ch, d, dsts):
        return [c for c in helpers(ch, d) + [R[(ch, d)]] if all(topo.may_write(c, x) for x in dsts)]

    for c in cores:
        load[c] = len([c2 for c2 in chips if topo.same_plane(topo.chip(c), c2)])

    landed = {}
    for i in range(NA):
        o = cores[i]
        ch, d = topo.chip(o), topo.die(o)
        sib = R[(ch, 1 - d)]
        same = [c2 for c2 in ring(ch) if topo.same_plane(ch, c2)]
        crs = [c2 for c2 in ring(ch) if not topo.same_plane(ch, c2)]
        direct = [R[(c2, d)] for c2 in same]
        load[o] += len(direct)
        for x in direct:
            landed.setdefault(x, []).append(i)
        feed = []
        for pd in (d, 1 - d):
            dsts = [R[(c2, pd)] for c2 in crs]
            for c, lst in share(dsts, gates(ch, pd, dsts)).items():
                if not lst:
                    continue
                if c == o:
                    direct = direct + lst
                elif c == sib:
                    add(sib, 2, i, 1, [("S", "S", lst, 0, 8)])
                else:
                    feed.append(c)
                    add(c, 2, i, 1, [("D", "S", lst, 0, 8)])
        loads.setdefault(o, []).append((i, "a"))
        avail[(o, i, "S")] = ("S%d" % i, 16)
        avail[(o, i, "D")] = ("D%d" % i, 16)
        add(o, 0, i, 1, [("D", "S", direct, 0, 8), ("D", "S", [sib], 8, 4), ("D", "D", feed, 12, 4)])

    for x, got in landed.items():
        sib = R[(topo.chip(x), 1 - topo.die(x))]
        got = sorted(got)
        a = 0
        while a < len(got):
            b = a
            while b + 1 < len(got) and got[b + 1] == got[b] + 1:
                b += 1
            add(x, 4, got[a], b - a + 1, [("S", "S", [sib], 0, FWD)])
            a = b + 1

    for j, o in enumerate(cores):
        t = slot[j]
        ch, d = topo.chip(o), topo.die(o)
        direct = [R[(c2, d)] for c2 in ring(ch) if topo.same_plane(ch, c2)]
        dsts = [R[(c2, d)] for c2 in ring(ch) if not topo.same_plane(ch, c2)]
        feed = []
        sh = share(dsts, gates(ch, d, dsts))
        for h in helpers(ch, d):
            while direct and load.get(h, PEN) + 1 < load[o]:
                load[h] = load.get(h, PEN) + 1
                load[o] -= 1
                sh.setdefault(h, []).append(direct.pop())
        for c, lst in sh.items():
            if not lst:
                continue
            if c == o:
                direct = direct + lst
            else:
                feed.append(c)
                add(c, 3, t, 1, [("D", "S", lst, 0, 8)])
        loads.setdefault(o, []).append((t, "b"))
        avail[(o, t, "S")] = ("S%d" % t, 16)
        avail[(o, t, "D")] = ("D%d" % t, 16)
        add(o, 1, t, 1, [("D", "S", direct, 0, 8), ("D", "D", feed, 8, 8)])

    waves, aorder = {}, {}
    for o in cores:
        ch, d = topo.chip(o), topo.die(o)
        k = plane_of[ch]
        sib = R[(ch, 1 - d)]
        add(o, 5, groups[(d, k)][0], groups[(d, k)][1], [("S", "S", [sib], 0, FWD)])
        add(o, 6, groups[(d, 1 - k)][0], groups[(d, 1 - k)][1], [("S", "S", [sib], 0, FWD)])
        waves[o] = [groups[(d, k)], groups[(d, 1 - k)], groups[(1 - d, k)], groups[(1 - d, 1 - k)]]
        aorder[o] = sorted(range(NA), key=lambda i: (plane_of[topo.chip(cores[i])] != k, i))
    return {"ops": ops, "avail": avail, "loads": loads, "waves": waves, "aorder": aorder, "blk": blk}


def rank_program(g, core, T, topo):
    key = tuple(T.cores)
    if key not in _CACHE:
        _CACHE[key] = _plan(list(T.cores), topo)
    P = _CACHE[key]
    avail = P["avail"]
    u8 = dt.uint8

    def codes(m, s0, n):
        if m == "S":
            return T.wc[:, s0 * W:(s0 + n) * W].bitcast(u8)
        return T["dc%d" % s0][:].bitcast(u8)

    def plane(m, s0, n):
        if m == "S":
            return T.ws[:, s0 * W:(s0 + n) * W]
        return T["dp%d" % s0][:]

    def engines(dsts, lo, ne):
        ok = None
        for x in dsts:
            ok = topo.mask(core, x) if ok is None else ok & topo.mask(core, x)
        bits = [b for b in range(16) if (ok >> b) & 1][lo:lo + ne]
        return sum(1 << b for b in bits)

    rank = T.rank_of(core)
    if rank is not None:
        src = {"a": (T.ac, T.az), "b": (T.bc, T.bs)}
        for (t, k) in P["loads"][core]:
            g.sync.dma_start(plane("D", t, 1), src[k][1][:, :]).then_inc(T.sem["pD%d" % t], 16)
            g.scalar.dma_start(codes("D", t, 1), src[k][0][:, :]).then_inc(T.sem["cD%d" % t], 16)
        g.scalar.dma_start(T.xt[:], T.x[:, :]).then_inc(T.sem.xl, 16)
        for n_, (t, k) in enumerate(P["loads"][core]):
            q = g.sync if n_ == 0 else g.scalar
            q.dma_start(codes("S", t, 1), src[k][0][:, :]).then_inc(T.sem["cS%d" % t], 16)
            g.sync.dma_start(plane("S", t, 1), src[k][1][:, :]).then_inc(T.sem["pS%d" % t], 16)

    seen, lcount = set(), 0
    for (prio, seq, s0, n, parts) in sorted(P["ops"].get(core, [])):
        for (vn, view) in (("p", plane), ("c", codes)):
            for (sm, dm, dsts, lo, ne) in parts:
                for t in range(s0, s0 + n):
                    sem, cnt = avail[(core, t, sm)]
                    if vn + sem not in seen:
                        seen.add(vn + sem)
                        g.wait_ge(T.sem[vn + sem], cnt)
            trs = []
            for (sm, dm, dsts, lo, ne) in parts:
                ids = []
                for x in dsts:
                    rid, pid, _se = topo.addr(x)
                    ids.append(DstId(rid=rid, pnc=pid))
                trs.append(RemoteDMATransfer(dst_ids=ids, dma_engine_mask=engines(dsts, lo, ne),
                                             remote_sem=T.sem[vn + dm + str(s0)], srcs=[view(sm, s0, n)],
                                             dsts=[view(dm, s0, n) for _x in dsts]))
                lcount += ne
            g.remote_dma_fused(trs, local_sem=T.sem.lsem)
    if lcount:
        g.wait_ge(T.sem.lsem, lcount)
    if rank is None:
        return

    v, sc, te = g.vector, g.scalar, g.tensor
    v.wait_ge(T.sem.xl, 16)
    v.quantize_mx(T.xq[:], T.xs[:], T.xt[:]).then_inc(T.sem.xqd, 1)
    te.wait_ge(T.sem.xqd, 1)
    tseen = set()

    def twait(t):
        sem, cnt = avail[(core, t, "S")]
        if sem not in tseen:
            tseen.add(sem)
            te.wait_ge(T.sem["p" + sem], cnt)
            te.wait_ge(T.sem["c" + sem], cnt)

    for n_, i in enumerate(P["aorder"][core]):
        twait(i)
        te.matmul_mx(T.ps[:, i * 512:i * 512 + W], T.wc[:, i * W:(i + 1) * W], T.ws[:, i * W:(i + 1) * W],
                     T.xq[:], T.xs[:], True, True).then_inc(T.sem["z%d" % i], 1)
        if n_ % 2 == 0:
            v.wait_ge(T.sem["z%d" % i], 1)
            v.tensor_scalar(T.ht[:, i:4 * W:4], T.ps[:, i * 512:i * 512 + W], 0.0, CSCALE,
                            AluOpType.max, AluOpType.mult).then_inc(T.sem.act, 1)
        else:
            sc.wait_ge(T.sem["z%d" % i], 1)
            sc.activation(T.ht[:, i:4 * W:4], T.ps[:, i * 512:i * 512 + W], ActivationFunctionType.Relu,
                          scale=CSCALE).then_inc(T.sem.act, 1)
    v.wait_ge(T.sem.act, NA)
    v.quantize_mx(T.hq[:], T.hs[:], T.ht[:]).then_inc(T.sem.hqd, 1)
    te.wait_ge(T.sem.hqd, 1)

    order, nst = [], 0
    for (s0, n) in P["waves"][core]:
        js = []
        for t in range(s0, s0 + n):
            j = P["blk"][t]
            k = len(order)
            bank = (NA + k) % 8
            twait(t)
            if k >= 8:
                te.wait_ge(T.sem["e%d" % order[k - 8]], 1)
            te.matmul_mx(T.ps[:, bank * 512:bank * 512 + W], T.wc[:, t * W:(t + 1) * W], T.ws[:, t * W:(t + 1) * W],
                         T.hq[:], T.hs[:], True, True).then_inc(T.sem["m%d" % j], 1)
            if k % 2 == 0:
                v.wait_ge(T.sem["m%d" % j], 1)
                v.tensor_copy(T.yo[:, j * W:(j + 1) * W], T.ps[:, bank * 512:bank * 512 + W]).then_inc(T.sem["e%d" % j], 1)
            else:
                sc.wait_ge(T.sem["m%d" % j], 1)
                sc.activation(T.yo[:, j * W:(j + 1) * W], T.ps[:, bank * 512:bank * 512 + W],
                              ActivationFunctionType.Copy).then_inc(T.sem["e%d" % j], 1)
            order.append(j)
            js.append(j)
        js.sort()
        a = 0
        while a < len(js):
            b = a
            while b + 1 < len(js) and js[b + 1] == js[b] + 1:
                b += 1
            for j in js[a:b + 1]:
                g.sync.wait_ge(T.sem["e%d" % j], 1)
            g.sync.dma_start(T.y[:, js[a] * W:(js[b] + 1) * W], T.yo[:, js[a] * W:(js[b] + 1) * W]).then_inc(T.sem.st, 16)
            nst += 1
            a = b + 1
    g.sync.wait_ge(T.sem.st, 16 * nst)
